import numpy as np
import ml_dtypes


def mxq(x, axis, fmt="e4m3"):
    dtype, down = {"e4m3": (ml_dtypes.float8_e4m3fn, 7), "e5m2": (ml_dtypes.float8_e5m2, 14)}[fmt]
    v = np.moveaxis(np.asarray(x, np.float32).astype(ml_dtypes.bfloat16).astype(np.float64), axis, -1)
    blocks = v.reshape(v.shape[:-1] + (-1, 32))
    amax = np.abs(blocks).max(-1, keepdims=True)
    byte = np.maximum(np.where(amax > 0, np.frexp(amax)[1] - 1 + 127, 0) - down, 1)
    scale = np.exp2(byte - 127.0)
    codes = (blocks / scale).astype(np.float32).astype(dtype).astype(np.float64)
    return np.moveaxis((codes * scale).reshape(v.shape), -1, axis)


WIDE = False


def mx_kscale(k):
    if not WIDE:
        return np.ones(k)
    levels = np.array([10, -10, 5, -5, 0])
    if k % 512:
        return np.exp2(np.random.permutation(np.resize(levels, k // 32))).repeat(32)
    a = np.empty((k // 512, 16))
    for p in range(k // 512):
        a[p, :8] = np.random.permutation(np.resize(levels, 8))
        for g in range(8):
            far = levels[np.abs(levels - a[p, g]) >= 10]
            a[p, g + 8] = far[np.random.randint(len(far))]
    return np.exp2(a.ravel()).repeat(32)


def f64(x):
    return np.asarray(x).astype(np.float64)


def striped(idx):
    return np.tile(np.asarray(idx).reshape(-1, 16).T, (8, 1)).astype(np.uint16)


def unstriped(offs):
    return offs[:16].T.reshape(-1).astype(np.int64)


E2M1 = np.array([0.0, 0.5, 1.0, 1.5, 2.0, 3.0, 4.0, 6.0, -0.0, -0.5, -1.0, -1.5, -2.0, -3.0, -4.0, -6.0])


def pack_weight(w, fmt):
    k, n = w.shape
    w = f64(np.asarray(w, np.float32).astype(ml_dtypes.bfloat16)).reshape(k // 32, 32, n)
    amax = np.abs(w).max(1)
    if fmt == "e4m3":
        byte = np.frexp(amax)[1] - 1 + 127 - 7
    else:
        mant, ex = np.frexp(amax / 6.0)
        byte = np.where(mant > 0.5, ex, ex - 1) + 127
    byte = np.clip(np.where(amax > 0, byte, 1), 1, 254)
    scaled = (w * np.exp2(127.0 - byte)[:, None, :]).reshape(k, n).astype(np.float32)
    by_word = np.ascontiguousarray(scaled.reshape(k // 512, 128, 4, n).transpose(0, 1, 3, 2))
    if fmt == "e4m3":
        words = by_word.astype(ml_dtypes.float8_e4m3fn).view(np.uint8)
    else:
        c = by_word.astype(ml_dtypes.float4_e2m1fn).view(np.uint8) & 0xF
        words = (c[..., 0::2] | (c[..., 1::2] << 4)).reshape(k // 512, 128, 2 * n)
    return np.ascontiguousarray(words), np.ascontiguousarray(byte.astype(np.uint8).reshape(k // 512, 16, n))


def unpack_weight(words, scales, fmt):
    g, _, n = scales.shape
    words = np.ascontiguousarray(words).reshape(g, 128, n, -1)
    if fmt == "e4m3":
        vals = words.view(ml_dtypes.float8_e4m3fn).astype(np.float64)
    else:
        nib = np.empty((g, 128, n, 4), np.uint8)
        nib[..., 0::2] = words & 0xF
        nib[..., 1::2] = words >> 4
        vals = E2M1[nib]
    vals = vals * np.repeat(np.exp2(scales.astype(np.float64) - 127.0), 8, axis=1)[..., None]
    return vals.transpose(0, 1, 3, 2).reshape(g * 512, n)


def sigmoid(v):
    return 1.0 / (1.0 + np.exp(-v))


D, E, T, I, Q, G, B = 512, 512, 2048, 512, 128, 64, 8


def setup_inputs():
    n = np.random.standard_normal
    idx = np.random.permutation(T)[:I]
    fd = mx_kscale(D)
    fe = mx_kscale(E)
    keysp = pack_weight(n((D, T)) / fd[:, None], "e2m1")
    valsp = pack_weight(n((E, T)) / fe[:, None], "e2m1")
    return {
        "query": (n((D, Q)) * 0.8 / np.sqrt(D) * fd[:, None]).astype(np.float32),
        "keys_words": keysp[0],
        "keys_scales": keysp[1],
        "steep": (np.random.uniform(2.0, 8.0, (Q, 1))).astype(np.float32),
        "gout": (n((E, Q)) * 1 / np.sqrt(E) * fe[:, None]).astype(np.float32),
        "vals_words": valsp[0],
        "vals_scales": valsp[1],
        "old": (0.5 * n((Q, T))).astype(np.float32),
        "offs": striped(idx),
    }


def reference(query, keys_words, keys_scales, steep, gout, vals_words, vals_scales, old, offs):
    idx = unstriped(offs)
    keysu = unpack_weight(keys_words, keys_scales, "e2m1")
    valsu = unpack_weight(vals_words, vals_scales, "e2m1")
    queryq = mxq(f64(query), 0, "e4m3")
    keysidxg = keysu[:, idx]
    a = queryq.T @ keysidxg
    m1 = a.reshape(Q, G, I // G).mean(axis=2)
    m2 = m1.reshape(Q, B, G // B).mean(axis=2)
    mr = np.repeat(m2, G // B, axis=1)
    g1 = sigmoid((m1 - mr) * f64(steep))
    gr = np.repeat(g1, I // G, axis=1)
    p = np.exp(a) * gr
    z = np.sum(p, axis=1, keepdims=True)
    goutq = mxq(f64(gout), 0, "e4m3")
    valsidxg = valsu[:, idx]
    c0 = goutq.T @ valsidxg
    dz = np.sum(c0 * p / np.square(z) * (-1.0), axis=1, keepdims=True)
    dp = c0 / z + dz
    dgr = dp * np.exp(a)
    dg1 = dgr.reshape(Q, G, I // G).sum(axis=2)
    dmr = dg1 * g1 * (1.0 - g1) * f64(steep) * (-1.0)
    dm2 = dmr.reshape(Q, B, G // B).sum(axis=2)
    e1 = dm2 / 8.0
    r1 = np.repeat(e1, G // B, axis=1)
    dm1 = dg1 * g1 * (1.0 - g1) * f64(steep) + r1
    e2 = dm1 / 8.0
    r2 = np.repeat(e2, I // G, axis=1)
    da = dp * gr * np.exp(a) + r2
    gs = da * 512.0
    gf = np.zeros((Q, T))
    gf[:, idx] = gs
    y = f64(old) + gf
    return y

@@ -1,0 +1,181 @@
+from contextlib import ExitStack
+
+import concourse.mybir as mybir
+
+F32 = mybir.dt.float32
+BF16 = mybir.dt.bfloat16
+I32 = mybir.dt.int32
+U32 = mybir.dt.uint32
+U16 = mybir.dt.uint16
+U8 = mybir.dt.uint8
+FP8X4 = mybir.dt.float8_e4m3fn_x4
+FP4X4 = mybir.dt.float4_e2m1fn_x4
+ALU = mybir.AluOpType
+ACT = mybir.ActivationFunctionType
+AX = mybir.AxisListType
+
+P = 128
+PACK = 4
+T = 2048
+SLOTS = 512
+GROUPS = 64
+BLOCKS = 8
+GSIZE = SLOTS // GROUPS
+BSIZE = GROUPS // BLOCKS
+OUT_WIDTHS = (256, 512, 512, 512, 256)
+
+FLOPS = 2 * 2 * 512 * 128 * 512
+
+
+def tile_attend_bblockcontrast_s_kernel(tc, query, keys_words, keys_scales, steep, gout, vals_words, vals_scales, old, offs, out):
+    nc = tc.nc
+    with ExitStack() as ctx:
+        sb = ctx.enter_context(tc.tile_pool(name="sb", bufs=1))
+        ps = ctx.enter_context(tc.psum_pool(name="ps", bufs=1))
+
+        offsets = sb.tile([P, SLOTS // 16], U16, name="offsets")
+        k_words = sb.tile([P, T], U16, name="k_words")
+        v_words = sb.tile([P, T], U16, name="v_words")
+        k_scales = sb.tile([P, T], U8, name="k_scales")
+        v_scales = sb.tile([P, T], U8, name="v_scales")
+        q_raw = sb.tile([P, PACK, P], F32, name="q_raw")
+        g_raw = sb.tile([P, PACK, P], F32, name="g_raw")
+        steep_col = sb.tile([P, 1], F32, name="steep_col")
+        old_sb = sb.tile([P, T], F32, name="old_sb")
+        window = sb.tile([P, T], F32, name="window")
+
+        nc.vector.memset(k_scales[:].bitcast(I32), 0)
+        nc.vector.memset(v_scales[:].bitcast(I32), 0)
+        nc.vector.memset(window[:], 0.0)
+
+        def load_scales(queue, dst, src):
+            for quad in range(4):
+                queue.dma_start(out=dst[32 * quad : 32 * quad + 4, :].bitcast(I32), in_=src[0, 4 * quad : 4 * quad + 4, :].bitcast(I32))
+
+        nc.sync.dma_start(offsets[:], offs)
+        nc.sync.dma_start(out=k_words[:].bitcast(I32), in_=keys_words[0].bitcast(I32))
+        load_scales(nc.scalar, k_scales, keys_scales)
+        nc.sync.dma_start(out=q_raw[:], in_=query.rearrange("(p j) w -> p j w", j=PACK))
+        nc.sync.dma_start(out=v_words[:].bitcast(I32), in_=vals_words[0].bitcast(I32))
+        nc.gpsimd.dma_start(out=steep_col[:], in_=steep)
+        nc.sync.dma_start(out=g_raw[:], in_=gout.rearrange("(p j) w -> p j w", j=PACK))
+        load_scales(nc.sync, v_scales, vals_scales)
+        nc.sync.dma_start(out=old_sb[:], in_=old)
+
+        def round_rows(raw, name):
+            grouped = sb.tile([P, P, PACK], BF16, name=name + "_bf", align_bytes=64)
+            nc.scalar.activation(grouped[:], raw[:].rearrange("p j w -> p w j"), ACT.Copy)
+            return grouped
+
+        def quantize(grouped, name):
+            codes = sb.tile([P, P], U32, name=name + "_codes", align_bytes=64)
+            plane = sb.tile([P, P], U8, name=name + "_plane", align_bytes=64)
+            nc.vector.quantize_mx(out=codes[:].bitcast(FP8X4), scales=plane[:], in_=grouped[:].rearrange("p w j -> p (w j)"))
+            return codes, plane
+
+        def gather(src, dtype, name, pieces):
+            dst = sb.tile([P, SLOTS], dtype, name=name, align_bytes=64)
+            n = SLOTS // pieces
+            for i in range(pieces):
+                nc.vector.tensor_copy(dst[:, i * n : (i + 1) * n], src[:].indirect(offsets[:, i * n // 16 : (i + 1) * n // 16]))
+            return dst
+
+        def product(name, codes, plane, words, scales):
+            acc = ps.tile([P, SLOTS], F32, name=name)
+            nc.tensor.matmul_mx(out=acc[:], lhsT=codes[:].bitcast(FP8X4), lhsT_scale=plane[:], rhs=words[:].bitcast(FP4X4), rhs_scale=scales[:], start=True, stop=True)
+            return acc
+
+        def small(name, width):
+            return sb.tile([P, width], F32, name=name)
+
+        def by_group(tile):
+            return tile[:].rearrange("p (g r) -> p g r", r=GSIZE)
+
+        def by_block(tile):
+            return tile[:].rearrange("p (b g) -> p b g", g=BSIZE)
+
+        def spread(tile, n):
+            return tile[:].unsqueeze(2).to_broadcast([P, tile[:].shape[1], n])
+
+        steep16 = small("steep16", 1)
+        steep32 = small("steep32", 1)
+        steep32n = small("steep32n", 1)
+        nc.gpsimd.tensor_scalar(steep16[:], steep_col[:], 1.0 / 16.0, 0.0, ALU.mult, ALU.add)
+        nc.gpsimd.tensor_scalar(steep32[:], steep_col[:], 32.0, 0.0, ALU.mult, ALU.add)
+        nc.gpsimd.tensor_scalar(steep32n[:], steep_col[:], -32.0, 0.0, ALU.mult, ALU.add)
+
+        q_bf = round_rows(q_raw, "q")
+        g_bf = round_rows(g_raw, "g")
+
+        kw = gather(k_words, U16, "kw", 1)
+        q_codes, q_plane = quantize(q_bf, "q")
+        ks = gather(k_scales, U8, "ks", 1)
+        a_ps = product("a_ps", q_codes, q_plane, kw, ks)
+
+        neg_a = small("neg_a", SLOTS)
+        neg_max = small("neg_max", 1)
+        nc.vector.tensor_scalar(neg_a[:], a_ps[:], -1.0, None, ALU.mult, ALU.min, accum_out=neg_max[:])
+        e = small("e", SLOTS)
+        nc.scalar.activation(e[:], neg_a[:], ACT.Exp, bias=neg_max[:], scale=-1.0)
+
+        neg_s1 = small("neg_s1", GROUPS)
+        nc.vector.tensor_reduce(neg_s1[:], by_group(neg_a), AX.X, ALU.add)
+        neg_s2 = small("neg_s2", BLOCKS)
+        nc.vector.tensor_reduce(neg_s2[:], by_block(neg_s1), AX.X, ALU.add)
+        diff = small("diff", GROUPS)
+        nc.vector.scalar_tensor_tensor(by_block(diff), spread(neg_s2, BSIZE), 1.0 / BSIZE, by_block(neg_s1), ALU.mult, ALU.subtract)
+        th = small("th", GROUPS)
+        nc.scalar.activation(th[:], diff[:], ACT.Tanh, scale=steep16[:])
+        slope = small("slope", GROUPS)
+        nc.scalar.activation(slope[:], th[:], ACT.Identity, bias=steep32[:], scale=steep32n[:])
+
+        se = small("se", GROUPS)
+        nc.vector.tensor_reduce(se[:], by_group(e), AX.X, ALU.add)
+        gse = small("gse", GROUPS)
+        z2 = small("z2", 1)
+        nc.vector.scalar_tensor_tensor(gse[:], th[:], 1.0, se[:], ALU.add, ALU.mult, accum_out=z2[:])
+        rz = small("rz", 1)
+        nc.vector.reciprocal(rz[:], z2[:])
+        gate_z = small("gate_z", GROUPS)
+        nc.vector.tensor_scalar(gate_z[:], th[:], 1.0, rz[:], ALU.add, ALU.mult)
+        mass = small("mass", GROUPS)
+        nc.vector.tensor_scalar(mass[:], gse[:], rz[:], None, ALU.mult)
+
+        vw = gather(v_words, U16, "vw", 2)
+        g_codes, g_plane = quantize(g_bf, "g")
+        vs = gather(v_scales, U8, "vs", 2)
+        c_ps = product("c_ps", g_codes, g_plane, vw, vs)
+
+        ce = small("ce", SLOTS)
+        nc.vector.tensor_tensor(ce[:], c_ps[:], e[:], ALU.mult)
+        sc = small("sc", GROUPS)
+        nc.vector.tensor_reduce(sc[:], by_group(ce), AX.X, ALU.add)
+        neg_asc = small("neg_asc", GROUPS)
+        neg_mu = small("neg_mu", 1)
+        nc.vector.scalar_tensor_tensor(neg_asc[:], sc[:], -1.0, gate_z[:], ALU.mult, ALU.mult, accum_out=neg_mu[:])
+        w = small("w", GROUPS)
+        nc.vector.scalar_tensor_tensor(w[:], mass[:], neg_mu[:], neg_asc[:], ALU.mult, ALU.subtract)
+        h = small("h", GROUPS)
+        nc.vector.tensor_tensor(h[:], w[:], slope[:], ALU.mult)
+        h_sum = small("h_sum", BLOCKS)
+        nc.vector.tensor_reduce(h_sum[:], by_block(h), AX.X, ALU.add)
+        shift = small("shift", GROUPS)
+        nc.vector.scalar_tensor_tensor(by_block(shift), spread(h_sum, BSIZE), -1.0 / BSIZE, by_block(h), ALU.mult, ALU.add)
+        shift_wide = small("shift_wide", SLOTS)
+        nc.scalar.activation(by_group(shift_wide), spread(shift, GSIZE), ACT.Copy)
+
+        prob = small("prob", SLOTS)
+        nc.vector.scalar_tensor_tensor(by_group(prob), by_group(e), 512.0, spread(gate_z, GSIZE), ALU.mult, ALU.mult)
+        direct = small("direct", SLOTS)
+        nc.vector.scalar_tensor_tensor(direct[:], c_ps[:], neg_mu[:], prob[:], ALU.add, ALU.mult)
+
+        nc.vector.tensor_tensor(window[:].indirect(offsets[:]), direct[:], shift_wide[:], ALU.add)
+
+        start = 0
+        for n, width in enumerate(OUT_WIDTHS):
+            cols = slice(start, start + width)
+            res = sb.tile([P, width], F32, name="res%d" % n)
+            nc.vector.tensor_tensor(res[:], window[:, cols], old_sb[:, cols], ALU.add)
+            queue = nc.sync if n % 2 == 0 else nc.scalar
+            queue.dma_start(out=out[:, cols], in_=res[:])
+            start = start + width

@@ -22,7 +22,7 @@ GROUPS = 64
 BLOCKS = 8
 GSIZE = SLOTS // GROUPS
 BSIZE = GROUPS // BLOCKS
-OUT_WIDTHS = (256, 512, 512, 512, 256)
+OUT_WIDTHS = ((512, 512), (512, 512))
 
 FLOPS = 2 * 2 * 512 * 128 * 512
 
@@ -38,10 +38,7 @@ def tile_attend_bblockcontrast_s_kernel(tc, query, keys_words, keys_scales, stee
         v_words = sb.tile([P, T], U16, name="v_words")
         k_scales = sb.tile([P, T], U8, name="k_scales")
         v_scales = sb.tile([P, T], U8, name="v_scales")
-        q_raw = sb.tile([P, PACK, P], F32, name="q_raw")
-        g_raw = sb.tile([P, PACK, P], F32, name="g_raw")
         steep_col = sb.tile([P, 1], F32, name="steep_col")
-        old_sb = sb.tile([P, T], F32, name="old_sb")
         window = sb.tile([P, T], F32, name="window")
 
         nc.vector.memset(k_scales[:].bitcast(I32), 0)
@@ -52,37 +49,29 @@ def tile_attend_bblockcontrast_s_kernel(tc, query, keys_words, keys_scales, stee
             for quad in range(4):
                 queue.dma_start(out=dst[32 * quad : 32 * quad + 4, :].bitcast(I32), in_=src[0, 4 * quad : 4 * quad + 4, :].bitcast(I32))
 
+        def load_rows(queue, src, name):
+            raw = sb.tile([P, PACK, P], F32, name=name, tag=name)
+            queue.dma_start(out=raw[:], in_=src.rearrange("(p j) w -> p j w", j=PACK))
+            return raw
+
         nc.sync.dma_start(offsets[:], offs)
         nc.sync.dma_start(out=k_words[:].bitcast(I32), in_=keys_words[0].bitcast(I32))
-        load_scales(nc.scalar, k_scales, keys_scales)
-        nc.sync.dma_start(out=q_raw[:], in_=query.rearrange("(p j) w -> p j w", j=PACK))
         nc.sync.dma_start(out=v_words[:].bitcast(I32), in_=vals_words[0].bitcast(I32))
+        q_raw = load_rows(nc.sync, query, "q_raw")
+        g_raw = load_rows(nc.sync, gout, "g_raw")
+        load_scales(nc.scalar, k_scales, keys_scales)
         nc.gpsimd.dma_start(out=steep_col[:], in_=steep)
-        nc.sync.dma_start(out=g_raw[:], in_=gout.rearrange("(p j) w -> p j w", j=PACK))
         load_scales(nc.sync, v_scales, vals_scales)
-        nc.sync.dma_start(out=old_sb[:], in_=old)
 
-        def round_rows(raw, name):
-            grouped = sb.tile([P, P, PACK], BF16, name=name + "_bf", align_bytes=64)
-            nc.scalar.activation(grouped[:], raw[:].rearrange("p j w -> p w j"), ACT.Copy)
-            return grouped
-
-        def quantize(grouped, name):
-            codes = sb.tile([P, P], U32, name=name + "_codes", align_bytes=64)
-            plane = sb.tile([P, P], U8, name=name + "_plane", align_bytes=64)
-            nc.vector.quantize_mx(out=codes[:].bitcast(FP8X4), scales=plane[:], in_=grouped[:].rearrange("p w j -> p (w j)"))
-            return codes, plane
-
-        def gather(src, dtype, name, pieces):
+        def gather(src, dtype, name):
             dst = sb.tile([P, SLOTS], dtype, name=name, align_bytes=64)
-            n = SLOTS // pieces
-            for i in range(pieces):
-                nc.vector.tensor_copy(dst[:, i * n : (i + 1) * n], src[:].indirect(offsets[:, i * n // 16 : (i + 1) * n // 16]))
+            nc.vector.tensor_copy(dst[:], src[:].indirect(offsets[:]))
             return dst
 
-        def product(name, codes, plane, words, scales):
+        def product(name, side, words, scales):
             acc = ps.tile([P, SLOTS], F32, name=name)
-            nc.tensor.matmul_mx(out=acc[:], lhsT=codes[:].bitcast(FP8X4), lhsT_scale=plane[:], rhs=words[:].bitcast(FP4X4), rhs_scale=scales[:], start=True, stop=True)
+            cols = slice(side * P, (side + 1) * P)
+            nc.tensor.matmul_mx(out=acc[:], lhsT=codes[:, cols].bitcast(FP8X4), lhsT_scale=plane[:, cols], rhs=words[:].bitcast(FP4X4), rhs_scale=scales[:], start=True, stop=True)
             return acc
 
         def small(name, width):
@@ -104,13 +93,19 @@ def tile_attend_bblockcontrast_s_kernel(tc, query, keys_words, keys_scales, stee
         nc.gpsimd.tensor_scalar(steep32[:], steep_col[:], 32.0, 0.0, ALU.mult, ALU.add)
         nc.gpsimd.tensor_scalar(steep32n[:], steep_col[:], -32.0, 0.0, ALU.mult, ALU.add)
 
-        q_bf = round_rows(q_raw, "q")
-        g_bf = round_rows(g_raw, "g")
+        rounded = sb.tile([P, 2, P, PACK], BF16, name="rounded", tag="rounded", align_bytes=64)
+        codes = sb.tile([P, 2 * P], U32, name="codes", align_bytes=64)
+        plane = sb.tile([P, 2 * P], U8, name="plane", align_bytes=64)
+        for side, raw in enumerate((q_raw, g_raw)):
+            nc.scalar.activation(rounded[:, side], raw[:].rearrange("p j w -> p w j"), ACT.Copy)
 
-        kw = gather(k_words, U16, "kw", 1)
-        q_codes, q_plane = quantize(q_bf, "q")
-        ks = gather(k_scales, U8, "ks", 1)
-        a_ps = product("a_ps", q_codes, q_plane, kw, ks)
+        kw = gather(k_words, U16, "kw")
+        vw = gather(v_words, U16, "vw")
+        ks = gather(k_scales, U8, "ks")
+        nc.vector.quantize_mx(out=codes[:].bitcast(FP8X4), scales=plane[:], in_=rounded[:].rearrange("p s w j -> p (s w j)"))
+        a_ps = product("a_ps", 0, kw, ks)
+        vs = gather(v_scales, U8, "vs")
+        c_ps = product("c_ps", 1, vw, vs)
 
         neg_a = small("neg_a", SLOTS)
         neg_max = small("neg_max", 1)
@@ -118,51 +113,55 @@ def tile_attend_bblockcontrast_s_kernel(tc, query, keys_words, keys_scales, stee
         e = small("e", SLOTS)
         nc.scalar.activation(e[:], neg_a[:], ACT.Exp, bias=neg_max[:], scale=-1.0)
 
-        neg_s1 = small("neg_s1", GROUPS)
-        nc.vector.tensor_reduce(neg_s1[:], by_group(neg_a), AX.X, ALU.add)
-        neg_s2 = small("neg_s2", BLOCKS)
-        nc.vector.tensor_reduce(neg_s2[:], by_block(neg_s1), AX.X, ALU.add)
+        s1 = small("s1", GROUPS)
+        nc.vector.tensor_reduce(s1[:], by_group(a_ps), AX.X, ALU.add)
+        s2 = small("s2", BLOCKS)
+        nc.vector.tensor_reduce(s2[:], by_block(s1), AX.X, ALU.add)
         diff = small("diff", GROUPS)
-        nc.vector.scalar_tensor_tensor(by_block(diff), spread(neg_s2, BSIZE), 1.0 / BSIZE, by_block(neg_s1), ALU.mult, ALU.subtract)
+        nc.vector.scalar_tensor_tensor(by_block(diff), spread(s2, BSIZE), -1.0 / BSIZE, by_block(s1), ALU.mult, ALU.add)
         th = small("th", GROUPS)
         nc.scalar.activation(th[:], diff[:], ACT.Tanh, scale=steep16[:])
         slope = small("slope", GROUPS)
         nc.scalar.activation(slope[:], th[:], ACT.Identity, bias=steep32[:], scale=steep32n[:])
+        th_sq = small("th_sq", GROUPS)
+        nc.scalar.activation(th_sq[:], th[:], ACT.Square)
+        curve = small("curve", GROUPS)
+        nc.scalar.activation(curve[:], th_sq[:], ACT.Identity, bias=steep32[:], scale=steep32n[:])
 
         se = small("se", GROUPS)
         nc.vector.tensor_reduce(se[:], by_group(e), AX.X, ALU.add)
-        gse = small("gse", GROUPS)
+        neg_ce = small("neg_ce", SLOTS)
+        nc.vector.scalar_tensor_tensor(neg_ce[:], c_ps[:], -1.0, e[:], ALU.mult, ALU.mult)
+
+        mass = small("mass", GROUPS)
         z2 = small("z2", 1)
-        nc.vector.scalar_tensor_tensor(gse[:], th[:], 1.0, se[:], ALU.add, ALU.mult, accum_out=z2[:])
+        nc.vector.scalar_tensor_tensor(mass[:], th[:], 1.0, se[:], ALU.add, ALU.mult, accum_out=z2[:])
         rz = small("rz", 1)
         nc.vector.reciprocal(rz[:], z2[:])
         gate_z = small("gate_z", GROUPS)
-        nc.vector.tensor_scalar(gate_z[:], th[:], 1.0, rz[:], ALU.add, ALU.mult)
-        mass = small("mass", GROUPS)
-        nc.vector.tensor_scalar(mass[:], gse[:], rz[:], None, ALU.mult)
+        nc.scalar.activation(gate_z[:], th[:], ACT.Identity, bias=rz[:], scale=rz[:])
+        rz_sq = small("rz_sq", 1)
+        nc.scalar.activation(rz_sq[:], rz[:], ACT.Square)
 
-        vw = gather(v_words, U16, "vw", 2)
-        g_codes, g_plane = quantize(g_bf, "g")
-        vs = gather(v_scales, U8, "vs", 2)
-        c_ps = product("c_ps", g_codes, g_plane, vw, vs)
-
-        ce = small("ce", SLOTS)
-        nc.vector.tensor_tensor(ce[:], c_ps[:], e[:], ALU.mult)
-        sc = small("sc", GROUPS)
-        nc.vector.tensor_reduce(sc[:], by_group(ce), AX.X, ALU.add)
-        neg_asc = small("neg_asc", GROUPS)
+        neg_sc = small("neg_sc", GROUPS)
+        nc.vector.tensor_reduce(neg_sc[:], by_group(neg_ce), AX.X, ALU.add)
+        mass_slope = small("mass_slope", GROUPS)
+        nc.vector.tensor_tensor(mass_slope[:], mass[:], slope[:], ALU.mult)
+        neg_sd = small("neg_sd", GROUPS)
+        neg_s = small("neg_s", 1)
+        nc.vector.scalar_tensor_tensor(neg_sd[:], th[:], 1.0, neg_sc[:], ALU.add, ALU.mult, accum_out=neg_s[:])
+        neg_scz = small("neg_scz", GROUPS)
+        nc.vector.scalar_tensor_tensor(neg_scz[:], neg_sc[:], z2[:], curve[:], ALU.mult, ALU.mult)
         neg_mu = small("neg_mu", 1)
-        nc.vector.scalar_tensor_tensor(neg_asc[:], sc[:], -1.0, gate_z[:], ALU.mult, ALU.mult, accum_out=neg_mu[:])
-        w = small("w", GROUPS)
-        nc.vector.scalar_tensor_tensor(w[:], mass[:], neg_mu[:], neg_asc[:], ALU.mult, ALU.subtract)
+        nc.scalar.activation(neg_mu[:], neg_s[:], ACT.Copy, scale=rz[:])
         h = small("h", GROUPS)
-        nc.vector.tensor_tensor(h[:], w[:], slope[:], ALU.mult)
+        nc.vector.scalar_tensor_tensor(h[:], mass_slope[:], neg_s[:], neg_scz[:], ALU.mult, ALU.subtract)
         h_sum = small("h_sum", BLOCKS)
         nc.vector.tensor_reduce(h_sum[:], by_block(h), AX.X, ALU.add)
         shift = small("shift", GROUPS)
         nc.vector.scalar_tensor_tensor(by_block(shift), spread(h_sum, BSIZE), -1.0 / BSIZE, by_block(h), ALU.mult, ALU.add)
         shift_wide = small("shift_wide", SLOTS)
-        nc.scalar.activation(by_group(shift_wide), spread(shift, GSIZE), ACT.Copy)
+        nc.scalar.activation(by_group(shift_wide), spread(shift, GSIZE), ACT.Copy, scale=rz_sq[:])
 
         prob = small("prob", SLOTS)
         nc.vector.scalar_tensor_tensor(by_group(prob), by_group(e), 512.0, spread(gate_z, GSIZE), ALU.mult, ALU.mult)
@@ -171,11 +170,23 @@ def tile_attend_bblockcontrast_s_kernel(tc, query, keys_words, keys_scales, stee
 
         nc.vector.tensor_tensor(window[:].indirect(offsets[:]), direct[:], shift_wide[:], ALU.add)
 
-        start = 0
-        for n, width in enumerate(OUT_WIDTHS):
-            cols = slice(start, start + width)
-            res = sb.tile([P, width], F32, name="res%d" % n)
-            nc.vector.tensor_tensor(res[:], window[:, cols], old_sb[:, cols], ALU.add)
-            queue = nc.sync if n % 2 == 0 else nc.scalar
-            queue.dma_start(out=out[:, cols], in_=res[:])
-            start = start + width
+        old_halves = []
+        for half, tag in enumerate(("g_raw", "rounded")):
+            if half == 0:
+                old_half = sb.tile([P, T // 2], F32, name="old0", tag=tag)
+            else:
+                old_half = sb.tile([P, T // 2], F32, name="old1", tag=tag, align_bytes=64)
+            nc.sync.dma_start(out=old_half[:], in_=old[:, half * T // 2 : (half + 1) * T // 2])
+            old_halves.append(old_half)
+
+        stores = 0
+        for half in range(2):
+            start = 0
+            for width in OUT_WIDTHS[half]:
+                cols = slice(half * T // 2 + start, half * T // 2 + start + width)
+                res = sb.tile([P, width], F32, name="res%d" % stores)
+                nc.vector.tensor_tensor(res[:], window[:, cols], old_halves[half][:, start : start + width], ALU.add)
+                queue = nc.sync if stores % 2 == 0 else nc.scalar
+                queue.dma_start(out=out[:, cols], in_=res[:])
+                start = start + width
+                stores = stores + 1

from contextlib import ExitStack

import concourse.mybir as mybir

F32 = mybir.dt.float32
BF16 = mybir.dt.bfloat16
I32 = mybir.dt.int32
U32 = mybir.dt.uint32
U16 = mybir.dt.uint16
U8 = mybir.dt.uint8
FP8X4 = mybir.dt.float8_e4m3fn_x4
FP4X4 = mybir.dt.float4_e2m1fn_x4
ALU = mybir.AluOpType
ACT = mybir.ActivationFunctionType
AX = mybir.AxisListType

P = 128
PACK = 4
T = 2048
SLOTS = 512
GROUPS = 64
BLOCKS = 8
GSIZE = SLOTS // GROUPS
BSIZE = GROUPS // BLOCKS
OUT_WIDTHS = ((512, 512), (512, 512))

FLOPS = 2 * 2 * 512 * 128 * 512


def tile_attend_bblockcontrast_s_kernel(tc, query, keys_words, keys_scales, steep, gout, vals_words, vals_scales, old, offs, out):
    nc = tc.nc
    with ExitStack() as ctx:
        sb = ctx.enter_context(tc.tile_pool(name="sb", bufs=1))
        ps = ctx.enter_context(tc.psum_pool(name="ps", bufs=1))

        offsets = sb.tile([P, SLOTS // 16], U16, name="offsets")
        k_words = sb.tile([P, T], U16, name="k_words")
        v_words = sb.tile([P, T], U16, name="v_words")
        k_scales = sb.tile([P, T], U8, name="k_scales")
        v_scales = sb.tile([P, T], U8, name="v_scales")
        steep_col = sb.tile([P, 1], F32, name="steep_col")
        window = sb.tile([P, T], F32, name="window")

        nc.vector.memset(k_scales[:].bitcast(I32), 0)
        nc.vector.memset(v_scales[:].bitcast(I32), 0)
        nc.vector.memset(window[:], 0.0)

        def load_scales(queue, dst, src):
            for quad in range(4):
                queue.dma_start(out=dst[32 * quad : 32 * quad + 4, :].bitcast(I32), in_=src[0, 4 * quad : 4 * quad + 4, :].bitcast(I32))

        def load_rows(queue, src, name):
            raw = sb.tile([P, PACK, P], F32, name=name, tag=name)
            queue.dma_start(out=raw[:], in_=src.rearrange("(p j) w -> p j w", j=PACK))
            return raw

        nc.sync.dma_start(offsets[:], offs)
        nc.sync.dma_start(out=k_words[:].bitcast(I32), in_=keys_words[0].bitcast(I32))
        nc.sync.dma_start(out=v_words[:].bitcast(I32), in_=vals_words[0].bitcast(I32))
        q_raw = load_rows(nc.sync, query, "q_raw")
        g_raw = load_rows(nc.sync, gout, "g_raw")
        load_scales(nc.scalar, k_scales, keys_scales)
        nc.gpsimd.dma_start(out=steep_col[:], in_=steep)
        load_scales(nc.sync, v_scales, vals_scales)

        def gather(src, dtype, name):
            dst = sb.tile([P, SLOTS], dtype, name=name, align_bytes=64)
            nc.vector.tensor_copy(dst[:], src[:].indirect(offsets[:]))
            return dst

        def product(name, side, words, scales):
            acc = ps.tile([P, SLOTS], F32, name=name)
            cols = slice(side * P, (side + 1) * P)
            nc.tensor.matmul_mx(out=acc[:], lhsT=codes[:, cols].bitcast(FP8X4), lhsT_scale=plane[:, cols], rhs=words[:].bitcast(FP4X4), rhs_scale=scales[:], start=True, stop=True)
            return acc

        def small(name, width):
            return sb.tile([P, width], F32, name=name)

        def by_group(tile):
            return tile[:].rearrange("p (g r) -> p g r", r=GSIZE)

        def by_block(tile):
            return tile[:].rearrange("p (b g) -> p b g", g=BSIZE)

        def spread(tile, n):
            return tile[:].unsqueeze(2).to_broadcast([P, tile[:].shape[1], n])

        steep16 = small("steep16", 1)
        steep32 = small("steep32", 1)
        steep32n = small("steep32n", 1)
        nc.gpsimd.tensor_scalar(steep16[:], steep_col[:], 1.0 / 16.0, 0.0, ALU.mult, ALU.add)
        nc.gpsimd.tensor_scalar(steep32[:], steep_col[:], 32.0, 0.0, ALU.mult, ALU.add)
        nc.gpsimd.tensor_scalar(steep32n[:], steep_col[:], -32.0, 0.0, ALU.mult, ALU.add)

        rounded = sb.tile([P, 2, P, PACK], BF16, name="rounded", tag="rounded", align_bytes=64)
        codes = sb.tile([P, 2 * P], U32, name="codes", align_bytes=64)
        plane = sb.tile([P, 2 * P], U8, name="plane", align_bytes=64)
        for side, raw in enumerate((q_raw, g_raw)):
            nc.scalar.activation(rounded[:, side], raw[:].rearrange("p j w -> p w j"), ACT.Copy)

        kw = gather(k_words, U16, "kw")
        vw = gather(v_words, U16, "vw")
        ks = gather(k_scales, U8, "ks")
        nc.vector.quantize_mx(out=codes[:].bitcast(FP8X4), scales=plane[:], in_=rounded[:].rearrange("p s w j -> p (s w j)"))
        a_ps = product("a_ps", 0, kw, ks)
        vs = gather(v_scales, U8, "vs")
        c_ps = product("c_ps", 1, vw, vs)

        neg_a = small("neg_a", SLOTS)
        neg_max = small("neg_max", 1)
        nc.vector.tensor_scalar(neg_a[:], a_ps[:], -1.0, None, ALU.mult, ALU.min, accum_out=neg_max[:])
        e = small("e", SLOTS)
        nc.scalar.activation(e[:], neg_a[:], ACT.Exp, bias=neg_max[:], scale=-1.0)

        s1 = small("s1", GROUPS)
        nc.vector.tensor_reduce(s1[:], by_group(a_ps), AX.X, ALU.add)
        s2 = small("s2", BLOCKS)
        nc.vector.tensor_reduce(s2[:], by_block(s1), AX.X, ALU.add)
        diff = small("diff", GROUPS)
        nc.vector.scalar_tensor_tensor(by_block(diff), spread(s2, BSIZE), -1.0 / BSIZE, by_block(s1), ALU.mult, ALU.add)
        th = small("th", GROUPS)
        nc.scalar.activation(th[:], diff[:], ACT.Tanh, scale=steep16[:])
        slope = small("slope", GROUPS)
        nc.scalar.activation(slope[:], th[:], ACT.Identity, bias=steep32[:], scale=steep32n[:])
        th_sq = small("th_sq", GROUPS)
        nc.scalar.activation(th_sq[:], th[:], ACT.Square)
        curve = small("curve", GROUPS)
        nc.scalar.activation(curve[:], th_sq[:], ACT.Identity, bias=steep32[:], scale=steep32n[:])

        se = small("se", GROUPS)
        nc.vector.tensor_reduce(se[:], by_group(e), AX.X, ALU.add)
        neg_ce = small("neg_ce", SLOTS)
        nc.vector.scalar_tensor_tensor(neg_ce[:], c_ps[:], -1.0, e[:], ALU.mult, ALU.mult)

        mass = small("mass", GROUPS)
        z2 = small("z2", 1)
        nc.vector.scalar_tensor_tensor(mass[:], th[:], 1.0, se[:], ALU.add, ALU.mult, accum_out=z2[:])
        rz = small("rz", 1)
        nc.vector.reciprocal(rz[:], z2[:])
        gate_z = small("gate_z", GROUPS)
        nc.scalar.activation(gate_z[:], th[:], ACT.Identity, bias=rz[:], scale=rz[:])
        rz_sq = small("rz_sq", 1)
        nc.scalar.activation(rz_sq[:], rz[:], ACT.Square)

        neg_sc = small("neg_sc", GROUPS)
        nc.vector.tensor_reduce(neg_sc[:], by_group(neg_ce), AX.X, ALU.add)
        mass_slope = small("mass_slope", GROUPS)
        nc.vector.tensor_tensor(mass_slope[:], mass[:], slope[:], ALU.mult)
        neg_sd = small("neg_sd", GROUPS)
        neg_s = small("neg_s", 1)
        nc.vector.scalar_tensor_tensor(neg_sd[:], th[:], 1.0, neg_sc[:], ALU.add, ALU.mult, accum_out=neg_s[:])
        neg_scz = small("neg_scz", GROUPS)
        nc.vector.scalar_tensor_tensor(neg_scz[:], neg_sc[:], z2[:], curve[:], ALU.mult, ALU.mult)
        neg_mu = small("neg_mu", 1)
        nc.scalar.activation(neg_mu[:], neg_s[:], ACT.Copy, scale=rz[:])
        h = small("h", GROUPS)
        nc.vector.scalar_tensor_tensor(h[:], mass_slope[:], neg_s[:], neg_scz[:], ALU.mult, ALU.subtract)
        h_sum = small("h_sum", BLOCKS)
        nc.vector.tensor_reduce(h_sum[:], by_block(h), AX.X, ALU.add)
        shift = small("shift", GROUPS)
        nc.vector.scalar_tensor_tensor(by_block(shift), spread(h_sum, BSIZE), -1.0 / BSIZE, by_block(h), ALU.mult, ALU.add)
        shift_wide = small("shift_wide", SLOTS)
        nc.scalar.activation(by_group(shift_wide), spread(shift, GSIZE), ACT.Copy, scale=rz_sq[:])

        prob = small("prob", SLOTS)
        nc.vector.scalar_tensor_tensor(by_group(prob), by_group(e), 512.0, spread(gate_z, GSIZE), ALU.mult, ALU.mult)
        direct = small("direct", SLOTS)
        nc.vector.scalar_tensor_tensor(direct[:], c_ps[:], neg_mu[:], prob[:], ALU.add, ALU.mult)

        nc.vector.tensor_tensor(window[:].indirect(offsets[:]), direct[:], shift_wide[:], ALU.add)

        old_halves = []
        for half, tag in enumerate(("g_raw", "rounded")):
            if half == 0:
                old_half = sb.tile([P, T // 2], F32, name="old0", tag=tag)
            else:
                old_half = sb.tile([P, T // 2], F32, name="old1", tag=tag, align_bytes=64)
            nc.sync.dma_start(out=old_half[:], in_=old[:, half * T // 2 : (half + 1) * T // 2])
            old_halves.append(old_half)

        stores = 0
        for half in range(2):
            start = 0
            for width in OUT_WIDTHS[half]:
                cols = slice(half * T // 2 + start, half * T // 2 + start + width)
                res = sb.tile([P, width], F32, name="res%d" % stores)
                nc.vector.tensor_tensor(res[:], window[:, cols], old_halves[half][:, start : start + width], ALU.add)
                queue = nc.sync if stores % 2 == 0 else nc.scalar
                queue.dma_start(out=out[:, cols], in_=res[:])
                start = start + width
                stores = stores + 1
